import numpy as np
import ml_dtypes


def mxq(x, axis, fmt="e4m3"):
    dtype, down = {"e4m3": (ml_dtypes.float8_e4m3fn, 7), "e5m2": (ml_dtypes.float8_e5m2, 14)}[fmt]
    v = np.moveaxis(np.asarray(x, np.float32).astype(ml_dtypes.bfloat16).astype(np.float64), axis, -1)
    blocks = v.reshape(v.shape[:-1] + (-1, 32))
    amax = np.abs(blocks).max(-1, keepdims=True)
    byte = np.maximum(np.where(amax > 0, np.frexp(amax)[1] - 1 + 127, 0) - down, 1)
    scale = np.exp2(byte - 127.0)
    codes = (blocks / scale).astype(np.float32).astype(dtype).astype(np.float64)
    return np.moveaxis((codes * scale).reshape(v.shape), -1, axis)


WIDE = False


def mx_kscale(k):
    if not WIDE:
        return np.ones(k)
    levels = np.array([10, -10, 5, -5, 0])
    if k % 512:
        return np.exp2(np.random.permutation(np.resize(levels, k // 32))).repeat(32)
    a = np.empty((k // 512, 16))
    for p in range(k // 512):
        a[p, :8] = np.random.permutation(np.resize(levels, 8))
        for g in range(8):
            far = levels[np.abs(levels - a[p, g]) >= 10]
            a[p, g + 8] = far[np.random.randint(len(far))]
    return np.exp2(a.ravel()).repeat(32)


def f64(x):
    return np.asarray(x).astype(np.float64)


def striped(idx):
    return np.tile(idx.reshape(-1, 16).T, (8, 1)).astype(np.uint16)


def unstriped(offs):
    return offs[:16].T.reshape(-1).astype(np.int64)


def pack_weight(w):
    k, n = w.shape
    w = f64(np.asarray(w, np.float32).astype(ml_dtypes.bfloat16)).reshape(k // 32, 32, n)
    amax = np.abs(w).max(1)
    byte = np.clip(np.where(amax > 0, np.frexp(amax)[1] - 1 + 127 - 7, 1), 1, 254)
    scaled = (w * np.exp2(127.0 - byte)[:, None, :]).reshape(k, n).astype(np.float32)
    words = np.ascontiguousarray(scaled.reshape(k // 512, 128, 4, n).transpose(0, 1, 3, 2)).astype(ml_dtypes.float8_e4m3fn).view(np.uint8)
    return words, np.ascontiguousarray(byte.astype(np.uint8).reshape(k // 512, 16, n))


def unpack_weight(words, scales):
    g, p, n, _ = words.shape
    vals = np.ascontiguousarray(words).view(ml_dtypes.float8_e4m3fn).astype(np.float64) * np.repeat(np.exp2(scales.astype(np.float64) - 127.0), 8, axis=1)[..., None]
    return vals.transpose(0, 1, 3, 2).reshape(g * 512, n)


E2M1 = np.array([0.0, 0.5, 1.0, 1.5, 2.0, 3.0, 4.0, 6.0, -0.0, -0.5, -1.0, -1.5, -2.0, -3.0, -4.0, -6.0])


def pack_fp4(w):
    k, n = w.shape
    w = f64(np.asarray(w, np.float32).astype(ml_dtypes.bfloat16)).reshape(k // 32, 32, n)
    amax = np.abs(w).max(1)
    mant, ex = np.frexp(amax / 6.0)
    byte = np.clip(np.where(amax > 0, np.where(mant > 0.5, ex, ex - 1) + 127, 1), 1, 254)
    scaled = (w * np.exp2(127.0 - byte)[:, None, :]).reshape(k, n).astype(np.float32)
    c = np.ascontiguousarray(scaled.reshape(k // 512, 128, 4, n).transpose(0, 1, 3, 2)).astype(ml_dtypes.float4_e2m1fn).view(np.uint8) & 0xF
    words = (c[..., 0::2] | (c[..., 1::2] << 4)).reshape(k // 512, 128, 2 * n)
    return np.ascontiguousarray(words), np.ascontiguousarray(byte.astype(np.uint8).reshape(k // 512, 16, n))


def unpack_fp4(words, scales):
    g, _, n = scales.shape
    words = np.ascontiguousarray(words).reshape(g, 128, n, 2)
    nib = np.empty((g, 128, n, 4), np.uint8)
    nib[..., 0::2] = words & 0xF
    nib[..., 1::2] = words >> 4
    vals = E2M1[nib] * np.repeat(np.exp2(scales.astype(np.float64) - 127.0), 8, axis=1)[..., None]
    return vals.transpose(0, 1, 3, 2).reshape(g * 512, n)


def planes(y):
    n, m = y.shape
    v = y.astype(np.float32).astype(ml_dtypes.bfloat16).astype(np.float64).reshape(n // 32, 32, m)
    top = np.abs(v).max(1)
    byte = np.clip(np.where(top > 0, np.frexp(top)[1] - 1 + 127 - 7, 1), 1, 254)
    codes = (v * np.exp2(127.0 - byte)[:, None, :]).reshape(n, m).astype(np.float32).astype(ml_dtypes.float8_e4m3fn).view(np.uint8)
    words = codes.reshape(n // 512, 128, 4, m).transpose(0, 1, 3, 2)
    return np.ascontiguousarray(words), np.ascontiguousarray(byte.astype(np.uint8).reshape(n // 512, 16, m))


K, T, S, N, H, W = 512, 2048, 512, 512, 512, 256


def setup_inputs():
    n = np.random.standard_normal
    s = mx_kscale(K)[:, None]
    u = mx_kscale(H)
    packed_xT = pack_weight(n((K, T)) * s)
    packed_w1 = pack_fp4(n((K, H)) / np.sqrt(K) / s)
    packed_w2 = pack_fp4(n((H, N)) / np.sqrt(H) / u[:, None])
    return {
        "x_words": packed_xT[0],
        "x_scales": packed_xT[1],
        "w1_words": packed_w1[0],
        "w1_scales": packed_w1[1],
        "tau": np.random.uniform(0.5, 1.2, (H, 1)).astype(np.float32),
        "gn": (np.random.uniform(0.5, 1.5, (H, 1)) * u[:, None]).astype(np.float32),
        "w2_words": packed_w2[0],
        "w2_scales": packed_w2[1],
        "offs": striped(np.random.permutation(T)[:S]),
        "n1": striped(np.random.permutation(S)),
        "n2": striped(np.random.permutation(S)),
        "n3": striped(np.random.permutation(S)[:W]),
        "n4": striped(np.random.permutation(S)[:W]),
    }


def reference(x_words, x_scales, w1_words, w1_scales, tau, gn, w2_words, w2_scales, offs, n1, n2, n3, n4):
    xq = unpack_weight(x_words, x_scales)[:, unstriped(offs)]
    y = unpack_fp4(w1_words, w1_scales).T @ xq
    sz = np.abs(y)
    ea = np.exp(-1.0 * (f64(tau) * sz[:, unstriped(n1)]))
    z = f64(gn) * ((y - y[:, unstriped(n2)]) * ea)
    h = unpack_fp4(w2_words, w2_scales).T @ mxq(z, 0, "e4m3")
    ra = y[:, unstriped(n4)] - (0.5 * h[:, unstriped(n3)])
    out = h.copy()
    out[:, unstriped(n3)] = ra
    return (out,) + planes(out)

from contextlib import ExitStack

import concourse.mybir as mybir

K, T, S, H, N, W = 512, 2048, 512, 512, 512, 256
FLOPS = 2 * K * H * S + 2 * H * N * S

F32 = mybir.dt.float32
BF16 = mybir.dt.bfloat16
I32 = mybir.dt.int32
U32 = mybir.dt.uint32
U16 = mybir.dt.uint16
U8 = mybir.dt.uint8
FP8X4 = mybir.dt.float8_e4m3fn_x4
FP4X4 = mybir.dt.float4_e2m1fn_x4
ACT = mybir.ActivationFunctionType
ALU = mybir.AluOpType

P = 128
PACK = 4
HALF = S // 2


def tile_picked_skipputbela_none_po_kernel(
    tc, x_words, x_scales, w1_words, w1_scales, tau, gn, w2_words, w2_scales, offs, n1, n2, n3, n4, out_0, out_1, out_2
):
    nc = tc.nc
    with ExitStack() as ctx:
        keep = ctx.enter_context(tc.tile_pool(name="keep", bufs=1))
        psum = ctx.enter_context(tc.psum_pool(name="psum", bufs=1))

        def sb(name, shape, dtype, tag=None):
            return keep.tile(shape, dtype, name=name, tag=tag or name, align_bytes=64)

        def cols(half):
            return slice(half * HALF, (half + 1) * HALF)

        def entries(lst, half):
            return lst[:, half * HALF // 16 : (half + 1) * HALF // 16]

        def load_scale_rows(engine, plane, scales, q):
            engine.dma_start(out=plane[32 * q : 32 * q + 4, :].bitcast(I32), in_=scales[0, 4 * q : 4 * q + 4, :].bitcast(I32))

        offs_sb = keep.tile([P, S // 16], U16, name="offs_sb")
        n1_sb = keep.tile([P, S // 16], U16, name="n1_sb")
        n2_sb = keep.tile([P, S // 16], U16, name="n2_sb")
        n3_sb = keep.tile([P, W // 16], U16, name="n3_sb")
        n4_sb = keep.tile([P, W // 16], U16, name="n4_sb")
        xw = sb("xw", [P, T], U32)
        xs = sb("xs", [P, T], U8)
        w1w_raw = sb("w1w_raw", [P, 2 * H], U8)
        ws_raw = sb("ws_raw", [P, H], U8)
        w2w_raw = sb("w2w_raw", [P, 2 * N], U8)
        tau_sb = sb("tau_sb", [P, PACK], F32)
        gn_sb = sb("gn_sb", [P, PACK], F32)
        neg_tau = sb("neg_tau", [P, PACK], F32)

        nc.vector.memset(xs[:].bitcast(I32), 0)
        nc.vector.memset(ws_raw[:].bitcast(I32), 0)

        for lst_sb, lst in ((offs_sb, offs), (n1_sb, n1), (n2_sb, n2), (n4_sb, n4), (n3_sb, n3)):
            nc.sync.dma_start(lst_sb[:], lst)
        nc.sync.dma_start(out=xw[:].bitcast(I32), in_=x_words[0].rearrange("p c r -> p (c r)").bitcast(I32))
        for q in range(4):
            load_scale_rows(nc.scalar, xs, x_scales, q)
        nc.gpsimd.dma_start(out=w1w_raw[:].bitcast(I32), in_=w1_words[0].bitcast(I32))
        for q in range(3):
            load_scale_rows(nc.sync, ws_raw, w1_scales, q)
        load_scale_rows(nc.gpsimd, ws_raw, w1_scales, 3)
        nc.gpsimd.dma_start(out=w2w_raw[:].bitcast(I32), in_=w2_words[0].bitcast(I32))
        nc.gpsimd.dma_start(out=tau_sb[:], in_=tau.rearrange("(p t) o -> p (t o)", t=PACK))
        nc.gpsimd.dma_start(out=gn_sb[:], in_=gn.rearrange("(p t) o -> p (t o)", t=PACK))

        w1w = sb("w1w", [P, 2 * H], U8)
        w1s = sb("w1s", [P, H], U8)
        w2w = sb("w2w", [P, 2 * N], U8)
        w2s = sb("w2s", [P, N], U8)

        def deal_words(dealt, raw):
            nc.scalar.copy(
                out=dealt[:].bitcast(U16).rearrange("p (t m) -> p m t", t=PACK),
                in_=raw[:].bitcast(U16).rearrange("p (m t) -> p m t", t=PACK),
            )

        def deal_scales(engine, dealt):
            engine.tensor_copy(
                out=dealt[:].rearrange("p (t m) -> p m t", t=PACK), in_=ws_raw[:].rearrange("p (m t) -> p m t", t=PACK)
            )

        deal_words(w1w, w1w_raw)
        deal_words(w2w, w2w_raw)
        xg = sb("xg", [P, S], U32)
        xgs = sb("xgs", [P, S], U8)
        nc.vector.tensor_copy(xgs[:], xs[:].indirect(offs_sb[:]))
        deal_scales(nc.vector, w1s)
        for half in range(2):
            nc.vector.tensor_copy(xg[:, cols(half)], xw[:].indirect(entries(offs_sb, half)))
        for q in range(4):
            load_scale_rows(nc.sync, ws_raw, w2_scales, q)
        nc.gpsimd.tensor_scalar(neg_tau[:], tau_sb[:], -1.0, 0.0, ALU.mult, ALU.add)
        deal_scales(nc.gpsimd, w2s)

        def product(words, scales, moving, moving_scales, t, half):
            acc = psum.tile([P, HALF], F32, name="acc", tag="bank%d%d" % (t, half))
            nc.tensor.matmul_mx(
                out=acc[:],
                lhsT=words[:, 2 * P * t : 2 * P * (t + 1)].bitcast(FP4X4),
                lhsT_scale=scales[:, P * t : P * (t + 1)],
                rhs=moving[:, cols(half)].bitcast(FP8X4),
                rhs_scale=moving_scales[:, cols(half)],
                start=True,
                stop=True,
            )
            return acc

        y_ps = {}
        for pair in range(2):
            for half in range(2):
                for t in (2 * pair, 2 * pair + 1):
                    y_ps[t, half] = product(w1w, w1s, xg, xgs, t, half)

        y = [sb("y%d" % t, [P, S], F32) for t in range(PACK)]
        sz = [sb("sz%d" % t, [P, S], F32) for t in range(PACK)]
        ea = [sb("ea%d" % h, [P, PACK, HALF], F32) for h in range(2)]
        g = [sb("g%d" % h, [P, PACK, HALF], F32) for h in range(2)]
        d = [sb("d%d" % h, [P, PACK, HALF], F32) for h in range(2)]
        zf = [sb("zf%d" % h, [P, PACK, HALF], F32) for h in range(2)]
        zb = [sb("zb%d" % h, [P, HALF, PACK], BF16) for h in range(2)]
        zq = sb("zq", [P, S], U32)
        zs = sb("zs", [P, S], U8)

        def size(t, half):
            nc.scalar.activation(sz[t][:, cols(half)], y_ps[t, half][:], ACT.Abs)

        def keep_y(t):
            for half in range(2):
                if t < 3:
                    nc.vector.tensor_copy(y[t][:, cols(half)], y_ps[t, half][:])
                else:
                    nc.scalar.copy(y[t][:, cols(half)], y_ps[t, half][:])

        def decay(t, half):
            nc.scalar.activation(
                ea[half][:, t, :], sz[t][:].indirect(entries(n1_sb, half)), ACT.Exp, scale=neg_tau[:, t : t + 1]
            )

        def fetch_v(t, half):
            nc.vector.tensor_copy(g[half][:, t, :], y[t][:].indirect(entries(n2_sb, half)))

        def fetch_s(t, half):
            nc.scalar.activation(g[half][:, t, :], y[t][:].indirect(entries(n2_sb, half)), ACT.Copy)

        def diff(t, half):
            nc.vector.tensor_tensor(d[half][:, t, :], y_ps[t, half][:], g[half][:, t, :], ALU.subtract)

        def gain(t, half):
            nc.vector.scalar_tensor_tensor(
                zf[half][:, t, :], d[half][:, t, :], gn_sb[:, t : t + 1], ea[half][:, t, :], ALU.mult, ALU.mult
            )

        def weave(half):
            nc.vector.tensor_copy(
                out=zb[half][:].rearrange("p (c i) t -> p c t i", i=4),
                in_=zf[half][:].rearrange("p t (c i) -> p c t i", i=4),
            )

        def quantise(half):
            nc.vector.quantize_mx(
                out=zq[:, cols(half)].bitcast(FP8X4),
                scales=zs[:, cols(half)],
                in_=zb[half][:].rearrange("p c t -> p (c t)"),
            )

        size(0, 0)
        size(1, 0)
        size(0, 1)
        keep_y(0)
        size(1, 1)
        keep_y(1)
        decay(0, 0)
        fetch_v(0, 0)
        size(2, 0)
        size(2, 1)
        keep_y(2)
        diff(0, 0)
        decay(1, 0)
        fetch_v(1, 0)
        size(3, 0)
        size(3, 1)
        keep_y(3)
        decay(2, 0)
        decay(3, 0)
        gain(0, 0)
        diff(1, 0)
        fetch_v(2, 0)
        gain(1, 0)
        fetch_v(3, 0)
        diff(2, 0)
        diff(3, 0)
        gain(2, 0)
        gain(3, 0)
        for t in range(PACK):
            fetch_s(t, 1)
            decay(t, 1)
        diff(0, 1)
        weave(0)
        gain(0, 1)
        quantise(0)
        h_ps = {}
        for t in range(PACK):
            h_ps[t, 0] = product(w2w, w2s, zq, zs, t, 0)
        for t in range(1, PACK):
            diff(t, 1)
            gain(t, 1)
        weave(1)
        quantise(1)
        for t in range(PACK):
            h_ps[t, 1] = product(w2w, w2s, zq, zs, t, 1)

        o = [sb("o%d" % t, [P, S], F32) for t in range(PACK)]
        y4 = sb("y4", [P, PACK, W], F32, tag="sz3")
        r = sb("r", [P, PACK, W], F32)
        pairs = sb("pairs", [P, 2, S, 2], BF16)
        ob = sb("ob", [P, S, PACK], BF16)
        oq = sb("oq", [P, S], U32)
        os_ = sb("os_", [P, S], U8)
        out_rows = out_0.rearrange("(p t) c -> p t c", t=PACK)

        for t in range(PACK):
            nc.scalar.activation(y4[:, t, :], y[t][:].indirect(n4_sb[:]), ACT.Copy, scale=2.0 if t % 2 == 0 else 1.0)
        for t in (0, 1):
            nc.scalar.copy(o[t][:, cols(0)], h_ps[t, 0][:])
        for t in (2, 3):
            nc.vector.tensor_copy(o[t][:, cols(0)], h_ps[t, 0][:])
        for t in (0, 1, 2):
            nc.scalar.copy(o[t][:, cols(1)], h_ps[t, 1][:])
        nc.scalar.activation(r[:, 1, :], o[1][:].indirect(n3_sb[:]), ACT.Copy, scale=-0.5)
        nc.scalar.copy(o[3][:, cols(1)], h_ps[3, 1][:])
        nc.scalar.activation(r[:, 3, :], o[3][:].indirect(n3_sb[:]), ACT.Copy, scale=-0.5)
        for t in (0, 2):
            nc.vector.tensor_tensor(r[:, t, :], o[t][:].indirect(n3_sb[:]), y4[:, t, :], ALU.subtract)
        for t in (0, 2):
            nc.scalar.activation(o[t][:].indirect(n3_sb[:]), r[:, t, :], ACT.Copy, scale=-0.5)
            nc.vector.tensor_tensor(o[t + 1][:].indirect(n3_sb[:]), r[:, t + 1, :], y4[:, t + 1, :], ALU.add)
        for t in (1, 0, 3, 2):
            nc.sync.dma_start(out=out_rows[:, t, :], in_=o[t][:])
        for t in (1, 3, 0, 2):
            nc.vector.tensor_copy(out=pairs[:, t // 2, :, t % 2], in_=o[t][:])
        pair_words = pairs[:].rearrange("p u c e -> p u (c e)").bitcast(I32)
        ob_words = ob[:].rearrange("p c t -> p (c t)").bitcast(I32)
        for half in range(2):
            nc.vector.tensor_copy(
                out=ob_words[:, 2 * half * HALF : 2 * (half + 1) * HALF].rearrange("p (c i u) -> p c u i", i=4, u=2),
                in_=pair_words[:, :, cols(half)].rearrange("p u (c i) -> p c u i", i=4),
            )
        words_out = out_1[0].rearrange("p c r -> p (c r)").bitcast(I32)
        for half in range(2):
            nc.vector.quantize_mx(
                out=oq[:, cols(half)].bitcast(FP8X4),
                scales=os_[:, cols(half)],
                in_=ob[:, cols(half), :].rearrange("p c t -> p (c t)"),
            )
            nc.sync.dma_start(out=words_out[:, cols(half)], in_=oq[:, cols(half)].bitcast(I32))
        for q in range(4):
            engine = nc.scalar if q % 2 == 0 else nc.sync
            engine.dma_start(out=out_2[0, 4 * q : 4 * q + 4, :].bitcast(I32), in_=os_[32 * q : 32 * q + 4, :].bitcast(I32))
